import numpy as np
import ml_dtypes


def mxq(x, axis, fmt="e4m3"):
    dtype, down = {"e4m3": (ml_dtypes.float8_e4m3fn, 7), "e5m2": (ml_dtypes.float8_e5m2, 14)}[fmt]
    v = np.moveaxis(np.asarray(x, np.float32).astype(ml_dtypes.bfloat16).astype(np.float64), axis, -1)
    blocks = v.reshape(v.shape[:-1] + (-1, 32))
    amax = np.abs(blocks).max(-1, keepdims=True)
    byte = np.maximum(np.where(amax > 0, np.frexp(amax)[1] - 1 + 127, 0) - down, 1)
    scale = np.exp2(byte - 127.0)
    codes = (blocks / scale).astype(np.float32).astype(dtype).astype(np.float64)
    return np.moveaxis((codes * scale).reshape(v.shape), -1, axis)


WIDE = False


def mx_kscale(k):
    if not WIDE:
        return np.ones(k)
    levels = np.array([10, -10, 5, -5, 0])
    if k % 512:
        return np.exp2(np.random.permutation(np.resize(levels, k // 32))).repeat(32)
    a = np.empty((k // 512, 16))
    for p in range(k // 512):
        a[p, :8] = np.random.permutation(np.resize(levels, 8))
        for g in range(8):
            far = levels[np.abs(levels - a[p, g]) >= 10]
            a[p, g + 8] = far[np.random.randint(len(far))]
    return np.exp2(a.ravel()).repeat(32)


BF16 = ml_dtypes.bfloat16


def bf(x):
    return np.asarray(x, np.float32).astype(BF16)


def f64(x):
    return np.asarray(x).astype(np.float64)


E2M1 = np.array([0.0, 0.5, 1.0, 1.5, 2.0, 3.0, 4.0, 6.0, -0.0, -0.5, -1.0, -1.5, -2.0, -3.0, -4.0, -6.0])


def pack_weight(w, fmt):
    k, n = w.shape
    w = f64(bf(w)).reshape(k // 32, 32, n)
    amax = np.abs(w).max(1)
    if fmt == "e4m3":
        byte = np.frexp(amax)[1] - 1 + 127 - 7
    else:
        mant, ex = np.frexp(amax / 6.0)
        byte = np.where(mant > 0.5, ex, ex - 1) + 127
    byte = np.clip(np.where(amax > 0, byte, 1), 1, 254)
    scaled = (w * np.exp2(127.0 - byte)[:, None, :]).reshape(k, n).astype(np.float32)
    by_word = np.ascontiguousarray(scaled.reshape(k // 512, 128, 4, n).transpose(0, 1, 3, 2))
    if fmt == "e4m3":
        words = by_word.astype(ml_dtypes.float8_e4m3fn).view(np.uint8)
    else:
        c = by_word.astype(ml_dtypes.float4_e2m1fn).view(np.uint8) & 0xF
        words = c[..., 0::2] | (c[..., 1::2] << 4)
    return np.ascontiguousarray(words), np.ascontiguousarray(byte.astype(np.uint8).reshape(k // 512, 16, n))


def unpack_weight(words, scales, fmt):
    g, p, n, _ = words.shape
    if fmt == "e4m3":
        vals = np.ascontiguousarray(words).view(ml_dtypes.float8_e4m3fn).astype(np.float64)
    else:
        nib = np.empty((g, p, n, 4), np.uint8)
        nib[..., 0::2] = words & 0xF
        nib[..., 1::2] = words >> 4
        vals = E2M1[nib]
    vals = vals * np.repeat(np.exp2(scales.astype(np.float64) - 127.0), 8, axis=1)[..., None]
    return vals.transpose(0, 1, 3, 2).reshape(g * 512, n)
def pack4(w):
    words, scales = pack_weight(w, "e2m1")
    return words.reshape(words.shape[0], 128, -1), scales


def unpack4(words, scales):
    return unpack_weight(words.reshape(words.shape[0], 128, -1, 2), scales, "e2m1")


def planes(Y):
    n, m = Y.shape
    b = f64(bf(Y)).reshape(n // 32, 32, m)
    amax = np.abs(b).max(1)
    byte = np.clip(np.where(amax > 0, np.frexp(amax)[1] - 1 + 127 - 7, 1), 1, 254)
    codes = (b * np.exp2(127.0 - byte)[:, None, :]).reshape(n, m).astype(np.float32).astype(ml_dtypes.float8_e4m3fn).view(np.uint8)
    words = codes.reshape(n // 512, 128, 4, m).transpose(0, 1, 3, 2)
    return np.ascontiguousarray(words), np.ascontiguousarray(byte.astype(np.uint8).reshape(n // 512, 16, m))


R, K, C, D = 4096, 1024, 512, 1024
COST_SPREAD, NOISE = 0.8, 0.4

def setup_inputs():
    s, t = mx_kscale(K), mx_kscale(R)
    phi_t = np.random.randn(K, R) * s[:, None]
    theta = COST_SPREAD * np.random.randn(K, C) / np.sqrt(K) / s[:, None]
    phi_words, phi_scales = pack4(phi_t)
    theta_words, theta_scales = pack4(theta)
    rollout_factor = np.exp(0.3 * np.random.randn(R)) * t
    eps = NOISE * np.random.randn(R, D) / np.sqrt(R) / t[:, None]
    return {
        "phi_words": phi_words, "phi_scales": phi_scales,
        "theta_words": theta_words, "theta_scales": theta_scales,
        "rollout_factor": bf(rollout_factor),
        "eps": bf(eps),
        "step": bf(1 + 0.2 * np.random.randn(C)),
        "nominal": bf(0.5 * np.random.randn(C, D)),
        "limit": bf(np.exp(0.8 * np.random.randn(D))),
    }

def reference(phi_words, phi_scales, theta_words, theta_scales, rollout_factor, eps, step, nominal, limit):
    phi_t = unpack4(phi_words, phi_scales)
    theta = unpack4(theta_words, theta_scales)
    cost = phi_t.T @ theta
    w = np.exp(-cost) * f64(rollout_factor)[:, None]
    wq = mxq(w, 0, "e4m3")
    eq = mxq(f64(eps), 0, "e4m3")
    update = wq.T @ eq
    y = f64(limit)[None, :] * np.tanh(f64(nominal) + f64(step)[:, None] * update)
    words, scales = planes(y.T)
    return y, words, scales

@@ -1,0 +1,306 @@
+from contextlib import ExitStack
+
+import concourse.mybir as mybir
+from concourse.masks import make_identity
+
+R, K, C, D = 4096, 1024, 512, 1024
+FLOPS = 2 * R * K * C + 2 * R * C * D
+
+F32 = mybir.dt.float32
+BF16 = mybir.dt.bfloat16
+I32 = mybir.dt.int32
+U32 = mybir.dt.uint32
+U8 = mybir.dt.uint8
+FP8X4 = mybir.dt.float8_e4m3fn_x4
+FP4X4 = mybir.dt.float4_e2m1fn_x4
+ACT = mybir.ActivationFunctionType
+ALU = mybir.AluOpType
+
+P = 128
+PACK = 4
+PASS = P * PACK
+K_PASSES = K // PASS
+GROUPS = R // PASS
+HALVES = D // PASS
+C_TILES = C // P
+EARLY_GROUPS = 2
+SCALAR_COLS = [192, 256, 256, 256, 256, 256, 256, 448, 384, 320, 384, 320, 256, 288, 192, 256]
+EPS_LAG = 2
+EPILOGUE_LAG = 2
+
+
+def tile_mppi_weighted_control_update_k5_kernel(
+    tc, phi_words, phi_scales, theta_words, theta_scales, rollout_factor, eps, step, nominal, limit,
+    out_0, out_1, out_2,
+):
+    nc = tc.nc
+    with ExitStack() as ctx:
+        keep = ctx.enter_context(tc.tile_pool(name="keep", bufs=1))
+        ring = ctx.enter_context(tc.tile_pool(name="ring", bufs=3))
+        psum = ctx.enter_context(tc.psum_pool(name="psum", bufs=1))
+        ctx.enter_context(tc.manual_schedule())
+
+        def kept(name, shape, dtype):
+            return keep.tile(shape, dtype, name=name, align_bytes=64)
+
+        def bank(index, shape):
+            return psum.tile(shape, F32, name="bank%d" % index)
+
+        theta_w = kept("theta_w", [P, K_PASSES, 2 * C], U8)
+        theta_s = kept("theta_s", [P, K_PASSES, C], U8)
+        scale_spans = [(0, EARLY_GROUPS), (EARLY_GROUPS, GROUPS)]
+        phi_s_raw = [
+            kept("phi_s_raw%d" % i, [P, K_PASSES, (g1 - g0) * PASS], U8) for i, (g0, g1) in enumerate(scale_spans)
+        ]
+        phi_w_raw = [kept("phi_w_raw%d" % g, [P, K_PASSES, 2 * PASS], U8) for g in range(GROUPS)]
+        eps_raw = [[kept("eps_raw%d_%d" % (h, g), [P, PACK, PASS], BF16) for g in range(GROUPS)] for h in range(HALVES)]
+        w_codes = [kept("w_codes%d" % g, [P, C], U32) for g in range(GROUPS)]
+        w_scales = [kept("w_scales%d" % g, [P, C], U8) for g in range(GROUPS)]
+        nominal_sb = [kept("nominal_sb%d" % h, [P, C_TILES, PASS], BF16) for h in range(HALVES)]
+        limit_sb = kept("limit_sb", [P, D], BF16)
+        y_codes = [kept("y_codes%d" % h, [P, C], U32) for h in range(HALVES)]
+        y_scales = [kept("y_scales%d" % h, [P, C], U8) for h in range(HALVES)]
+        small_raw = kept("small_raw", [P, PASS], BF16)
+        rows = kept("rows", [P, PACK, P], F32)
+        columns = kept("columns", [P, PACK, GROUPS], F32)
+        step_sb = kept("step_sb", [P, C_TILES, 2], BF16)
+        identity = kept("identity", [P, P], F32)
+        warm = kept("warm", [P, 2], F32)
+
+        nc.vector.memset(warm[:, 0:1], 1.0)
+        nc.vector.memset(phi_s_raw[0][:].rearrange("p k n -> p (k n)").bitcast(I32), 0)
+        nc.vector.memset(theta_s[:].rearrange("p k n -> p (k n)").bitcast(I32), 0)
+        nc.vector.memset(rows[:], 0.0)
+        nc.vector.memset(phi_s_raw[1][:].rearrange("p k n -> p (k n)").bitcast(I32), 0)
+
+        def load_scale_rows(plane, source):
+            for quadrant in range(4):
+                nc.sync.dma_start(
+                    out=plane[32 * quadrant : 32 * quadrant + 4, :, :].bitcast(I32),
+                    in_=source[:, 4 * quadrant : 4 * quadrant + 4, :].rearrange("k r n -> r k n").bitcast(I32),
+                )
+
+        def load_phi_words(g):
+            nc.sync.dma_start(
+                out=phi_w_raw[g][:].bitcast(I32),
+                in_=phi_words[:, :, 2 * PASS * g : 2 * PASS * (g + 1)].rearrange("k p n -> p k n").bitcast(I32),
+            )
+
+        def load_eps(h, g):
+            source = eps[PASS * g : PASS * (g + 1), PASS * h : PASS * (h + 1)].rearrange(
+                "(q t j) d -> j q t d", t=PACK, j=4
+            )
+            for j in range(4):
+                nc.sync.dma_start(out=eps_raw[h][g][j:P:4, :, :], in_=source[j])
+
+        def load_nominal(h):
+            nc.sync.dma_start(
+                out=nominal_sb[h][:], in_=nominal[:, PASS * h : PASS * (h + 1)].rearrange("(m p) d -> p m d", p=P)
+            )
+
+        make_identity(nc, identity[:])
+        eps_order = [(h, g) for h in range(HALVES) for g in range(GROUPS)]
+        nc.sync.dma_start(out=small_raw[0:GROUPS, :], in_=rollout_factor.rearrange("(g n) -> g n", g=GROUPS))
+        load_phi_words(0)
+        load_scale_rows(phi_s_raw[0], phi_scales[:, :, 0 : EARLY_GROUPS * PASS])
+        nc.sync.dma_start(out=theta_w[:].bitcast(I32), in_=theta_words.rearrange("k p n -> p k n").bitcast(I32))
+        load_scale_rows(theta_s, theta_scales)
+        load_phi_words(1)
+        load_scale_rows(phi_s_raw[1], phi_scales[:, :, EARLY_GROUPS * PASS :])
+        for e, (h, g) in enumerate(eps_order):
+            if e + EPS_LAG < GROUPS:
+                load_phi_words(e + EPS_LAG)
+            if e == GROUPS + 1:
+                load_nominal(0)
+                with nc.allow_non_contiguous_dma(reason="one step value for each partition"):
+                    nc.sync.dma_start(out=step_sb[:, :, 0:1], in_=step.rearrange("(m p o) -> p m o", p=P, o=1))
+                nc.sync.dma_start(out=limit_sb[:], in_=limit.partition_broadcast(P))
+            load_eps(h, g)
+        load_nominal(1)
+
+        nc.scalar.activation(out=warm[:, 1:2], in_=warm[:, 0:1], func=ACT.Ln)
+        nc.scalar.activation(
+            out=rows[0:GROUPS, :, :].rearrange("g t (q j) -> g t q j", j=4),
+            in_=small_raw[0:GROUPS, :].rearrange("g (q t j) -> g t q j", t=PACK, j=4),
+            func=ACT.Ln,
+        )
+        nc.scalar.activation(out=warm[:, 1:2], in_=warm[:, 0:1], func=ACT.Exp)
+        turned = bank(4, [P, PACK, P])
+        for t in range(PACK):
+            nc.tensor.transpose(turned[:, t, :], rows[:, t, :], identity[:])
+
+        phi_w, phi_s, eps_codes, eps_scales = {}, {}, {}, {}
+
+        def permute_phi(g):
+            phi_w[g] = ring.tile([P, PACK, K_PASSES, 2 * P], U8, name="phi_w", align_bytes=64)
+            phi_s[g] = ring.tile([P, PACK, K_PASSES, P], U8, name="phi_s", align_bytes=64)
+            nc.vector.tensor_copy(
+                out=phi_w[g][:].rearrange("p t k n -> p (t k n)").bitcast(I32).rearrange(
+                    "p (t u w) -> p u t w", t=PACK, w=2
+                ),
+                in_=phi_w_raw[g][:].rearrange("p k n -> p (k n)").bitcast(I32).rearrange(
+                    "p (u t w) -> p u t w", t=PACK, w=2
+                ),
+            )
+            span = 0 if g < EARLY_GROUPS else 1
+            first = (g - scale_spans[span][0]) * PASS
+            nc.vector.tensor_copy(
+                out=phi_s[g][:].bitcast(I32).rearrange("p t k q -> p k q t"),
+                in_=phi_s_raw[span][:, :, first : first + PASS].bitcast(I32).rearrange("p k (q t) -> p k q t", t=PACK),
+            )
+
+        def interleave(copy, grouped, raw, c0, c1):
+            copy(
+                out=grouped[:, c0:c1, :].rearrange("p (c i) t -> p c t i", i=4),
+                in_=raw[:, :, c0:c1].rearrange("p t (c i) -> p c t i", i=4),
+            )
+
+        def quantize(codes, scales, grouped):
+            nc.vector.quantize_mx(
+                out=codes.bitcast(FP8X4), scales=scales, in_=grouped[:].rearrange("p c t -> p (c t)")
+            )
+
+        eps_grouped, w_raw, w_grouped, update, squashed, y, y_turned, y_grouped = {}, {}, {}, {}, {}, {}, {}, {}
+
+        def interleave_eps(h, g):
+            grouped = ring.tile([P, PASS, PACK], BF16, name="eps_grouped", align_bytes=64)
+            split = SCALAR_COLS[GROUPS * h + g]
+            if split > 0:
+                interleave(nc.scalar.copy, grouped, eps_raw[h][g], 0, split)
+            interleave(nc.vector.tensor_copy, grouped, eps_raw[h][g], split, PASS)
+            eps_grouped[h, g] = grouped
+
+        def quantize_eps(h, g):
+            eps_codes[h, g] = ring.tile([P, PASS], U32, name="eps_codes", bufs=4, align_bytes=64)
+            eps_scales[h, g] = ring.tile([P, PASS], U8, name="eps_scales", bufs=4, align_bytes=64)
+            quantize(eps_codes[h, g][:], eps_scales[h, g][:], eps_grouped[h, g])
+
+        def weights(g):
+            raw = ring.tile([P, PACK, C], BF16, name="w_raw", align_bytes=64)
+            for t in range(PACK):
+                cost = bank(t, [P, C])
+                for k in range(K_PASSES):
+                    nc.tensor.matmul_mx(
+                        out=cost[:],
+                        lhsT=phi_w[g][:, t, k, :].bitcast(FP4X4),
+                        lhsT_scale=phi_s[g][:, t, k, :],
+                        rhs=theta_w[:, k, :].bitcast(FP4X4),
+                        rhs_scale=theta_s[:, k, :],
+                        start=(k == 0),
+                        stop=(k == K_PASSES - 1),
+                    )
+                nc.scalar.activation(
+                    out=raw[:, t, :], in_=cost[:], func=ACT.Exp, scale=-1.0, bias=columns[:, t, g : g + 1]
+                )
+            w_raw[g] = raw
+
+        def interleave_w(g):
+            grouped = ring.tile([P, C, PACK], BF16, name="w_grouped", align_bytes=64)
+            interleave(nc.vector.tensor_copy, grouped, w_raw[g], 0, C)
+            w_grouped[g] = grouped
+
+        def quantize_w(g):
+            quantize(w_codes[g][:], w_scales[g][:], w_grouped[g])
+
+        def accumulate(h, g):
+            for m in range(C_TILES):
+                if g == 0:
+                    update[h, m] = bank(m + 4 * (1 - h), [P, PASS])
+                goals = slice(P * m, P * (m + 1))
+                nc.tensor.matmul_mx(
+                    out=update[h, m][:],
+                    lhsT=w_codes[g][:, goals].bitcast(FP8X4),
+                    lhsT_scale=w_scales[g][:, goals],
+                    rhs=eps_codes[h, g][:].bitcast(FP8X4),
+                    rhs_scale=eps_scales[h, g][:],
+                    start=(g == 0),
+                    stop=(g == GROUPS - 1),
+                )
+
+        def squash(h, m):
+            plan = ring.tile([P, PASS], F32, name="plan")
+            nc.vector.scalar_tensor_tensor(
+                out=plan[:],
+                in0=update[h, m][:],
+                scalar=step_sb[:, m, 0:1],
+                in1=nominal_sb[h][:, m, :],
+                op0=ALU.mult,
+                op1=ALU.add,
+            )
+            squashed[h, m] = ring.tile([P, PASS], F32, name="squashed")
+            nc.scalar.activation(out=squashed[h, m][:], in_=plan[:], func=ACT.Tanh)
+
+        def scale_and_turn(h, m):
+            y[h, m] = kept("y%d_%d" % (h, m), [P, PASS], F32)
+            controls = slice(PASS * h, PASS * (h + 1))
+            nc.vector.tensor_tensor(out=y[h, m][:], in0=squashed[h, m][:], in1=limit_sb[:, controls], op=ALU.mult)
+            nc.sync.dma_start(out=out_0[P * m : P * (m + 1), controls], in_=y[h, m][:])
+            y_turned[h, m] = bank(4 + m, [P, PACK, P])
+            for t in range(PACK):
+                nc.tensor.transpose(y_turned[h, m][:, t, :], y[h, m][:, t:PASS:PACK], identity[:])
+
+        def round_y(h, m):
+            y_grouped[h, m] = ring.tile([P, P, PACK], BF16, name="y_grouped", align_bytes=64)
+            nc.scalar.copy(out=y_grouped[h, m][:], in_=y_turned[h, m][:].rearrange("p t c -> p c t"))
+
+        def quantize_y(h, m):
+            goals = slice(P * m, P * (m + 1))
+            quantize(y_codes[h][:, goals], y_scales[h][:, goals], y_grouped[h, m])
+
+        def store_words(h, m0, m1):
+            nc.sync.dma_start(
+                out=out_1[h, :, P * m0 : P * m1, :].rearrange("p m t -> p (m t)").bitcast(I32),
+                in_=y_codes[h][:, P * m0 : P * m1].bitcast(I32),
+            )
+
+        def store_scales(h, queues):
+            for quadrant in range(4):
+                queues[quadrant % len(queues)].dma_start(
+                    out=out_2[h, 4 * quadrant : 4 * quadrant + 4, :].bitcast(I32),
+                    in_=y_scales[h][32 * quadrant : 32 * quadrant + 4, :].bitcast(I32),
+                )
+
+        permute_phi(0)
+        nc.vector.tensor_copy(out=columns[:], in_=turned[:, :, 0:GROUPS])
+        accumulated = 0
+        for s in range(len(eps_order) + EPS_LAG):
+            e = s - EPS_LAG
+            m = e - GROUPS - EPILOGUE_LAG
+            if s < GROUPS:
+                weights(s)
+            if s + 1 < GROUPS:
+                permute_phi(s + 1)
+            if 0 <= m < C_TILES:
+                squash(0, m)
+            if e >= 0:
+                quantize_eps(*eps_order[e])
+            if 1 <= s <= GROUPS:
+                interleave_w(s - 1)
+            if 0 <= e + 1 < len(eps_order):
+                interleave_eps(*eps_order[e + 1])
+            if 1 <= s <= GROUPS:
+                quantize_w(s - 1)
+            while accumulated <= (e - 1 if s < GROUPS else e):
+                accumulate(*eps_order[accumulated])
+                accumulated += 1
+            if 0 <= m < C_TILES:
+                scale_and_turn(0, m)
+            if 1 <= m <= C_TILES:
+                round_y(0, m - 1)
+            if m >= 2:
+                quantize_y(0, m - 2)
+        store_words(0, 0, C_TILES)
+        store_scales(0, [nc.sync])
+        for s in range(C_TILES + 3):
+            if s < C_TILES:
+                squash(1, s)
+            if 1 <= s <= C_TILES:
+                scale_and_turn(1, s - 1)
+            if 2 <= s <= C_TILES + 1:
+                round_y(1, s - 2)
+            if s >= 3:
+                quantize_y(1, s - 3)
+            if s == C_TILES + 1:
+                store_words(1, 0, C_TILES - 1)
+        store_words(1, C_TILES - 1, C_TILES)
+        store_scales(1, [nc.scalar, nc.sync])

@@ -23,10 +23,10 @@ K_PASSES = K // PASS
 GROUPS = R // PASS
 HALVES = D // PASS
 C_TILES = C // P
-EARLY_GROUPS = 2
-SCALAR_COLS = [192, 256, 256, 256, 256, 256, 256, 448, 384, 320, 384, 320, 256, 288, 192, 256]
-EPS_LAG = 2
-EPILOGUE_LAG = 2
+EARLY_GROUPS = 3
+PHI_SPANS = [(0, 1), (1, 2), (2, 3), (3, 4), (4, 6), (6, 8)]
+SCALAR_COLS = [0, 64, 256, 256, 256, 256, 256, 256, 352, 352, 320, 320, 384, 352, 352, 320]
+LAG = 2
 
 
 def tile_mppi_weighted_control_update_k5_kernel(
@@ -52,7 +52,9 @@ def tile_mppi_weighted_control_update_k5_kernel(
         phi_s_raw = [
             kept("phi_s_raw%d" % i, [P, K_PASSES, (g1 - g0) * PASS], U8) for i, (g0, g1) in enumerate(scale_spans)
         ]
-        phi_w_raw = [kept("phi_w_raw%d" % g, [P, K_PASSES, 2 * PASS], U8) for g in range(GROUPS)]
+        phi_w_raw = [
+            kept("phi_w_raw%d" % g0, [P, K_PASSES, 2 * PASS * (g1 - g0)], U8) for g0, g1 in PHI_SPANS
+        ]
         eps_raw = [[kept("eps_raw%d_%d" % (h, g), [P, PACK, PASS], BF16) for g in range(GROUPS)] for h in range(HALVES)]
         w_codes = [kept("w_codes%d" % g, [P, C], U32) for g in range(GROUPS)]
         w_scales = [kept("w_scales%d" % g, [P, C], U8) for g in range(GROUPS)]
@@ -60,6 +62,7 @@ def tile_mppi_weighted_control_update_k5_kernel(
         limit_sb = kept("limit_sb", [P, D], BF16)
         y_codes = [kept("y_codes%d" % h, [P, C], U32) for h in range(HALVES)]
         y_scales = [kept("y_scales%d" % h, [P, C], U8) for h in range(HALVES)]
+        y_grouped = [kept("y_grouped%d" % h, [P, C, PACK], BF16) for h in range(HALVES)]
         small_raw = kept("small_raw", [P, PASS], BF16)
         rows = kept("rows", [P, PACK, P], F32)
         columns = kept("columns", [P, PACK, GROUPS], F32)
@@ -80,10 +83,11 @@ def tile_mppi_weighted_control_update_k5_kernel(
                     in_=source[:, 4 * quadrant : 4 * quadrant + 4, :].rearrange("k r n -> r k n").bitcast(I32),
                 )
 
-        def load_phi_words(g):
+        def load_phi_words(i):
+            g0, g1 = PHI_SPANS[i]
             nc.sync.dma_start(
-                out=phi_w_raw[g][:].bitcast(I32),
-                in_=phi_words[:, :, 2 * PASS * g : 2 * PASS * (g + 1)].rearrange("k p n -> p k n").bitcast(I32),
+                out=phi_w_raw[i][:].bitcast(I32),
+                in_=phi_words[:, :, 2 * PASS * g0 : 2 * PASS * g1].rearrange("k p n -> p k n").bitcast(I32),
             )
 
         def load_eps(h, g):
@@ -106,10 +110,12 @@ def tile_mppi_weighted_control_update_k5_kernel(
         nc.sync.dma_start(out=theta_w[:].bitcast(I32), in_=theta_words.rearrange("k p n -> p k n").bitcast(I32))
         load_scale_rows(theta_s, theta_scales)
         load_phi_words(1)
-        load_scale_rows(phi_s_raw[1], phi_scales[:, :, EARLY_GROUPS * PASS :])
+        phi_before = {1: 2, 2: 3, 3: 4, 5: 5}
         for e, (h, g) in enumerate(eps_order):
-            if e + EPS_LAG < GROUPS:
-                load_phi_words(e + EPS_LAG)
+            if e == 2:
+                load_scale_rows(phi_s_raw[1], phi_scales[:, :, EARLY_GROUPS * PASS :])
+            if e in phi_before:
+                load_phi_words(phi_before[e])
             if e == GROUPS + 1:
                 load_nominal(0)
                 with nc.allow_non_contiguous_dma(reason="one step value for each partition"):
@@ -131,23 +137,29 @@ def tile_mppi_weighted_control_update_k5_kernel(
 
         phi_w, phi_s, eps_codes, eps_scales = {}, {}, {}, {}
 
-        def permute_phi(g):
-            phi_w[g] = ring.tile([P, PACK, K_PASSES, 2 * P], U8, name="phi_w", align_bytes=64)
-            phi_s[g] = ring.tile([P, PACK, K_PASSES, P], U8, name="phi_s", align_bytes=64)
+        def permute_phi(i):
+            g0, g1 = PHI_SPANS[i]
+            words = ring.tile([P, PACK, K_PASSES, 2 * P * (g1 - g0)], U8, name="phi_w", align_bytes=64)
+            scales = ring.tile([P, PACK, K_PASSES, P * (g1 - g0)], U8, name="phi_s", align_bytes=64)
             nc.vector.tensor_copy(
-                out=phi_w[g][:].rearrange("p t k n -> p (t k n)").bitcast(I32).rearrange(
+                out=words[:].rearrange("p t k n -> p (t k n)").bitcast(I32).rearrange(
                     "p (t u w) -> p u t w", t=PACK, w=2
                 ),
-                in_=phi_w_raw[g][:].rearrange("p k n -> p (k n)").bitcast(I32).rearrange(
+                in_=phi_w_raw[i][:].rearrange("p k n -> p (k n)").bitcast(I32).rearrange(
                     "p (u t w) -> p u t w", t=PACK, w=2
                 ),
             )
-            span = 0 if g < EARLY_GROUPS else 1
-            first = (g - scale_spans[span][0]) * PASS
+            part = 0 if g0 < EARLY_GROUPS else 1
+            first = (g0 - scale_spans[part][0]) * PASS
             nc.vector.tensor_copy(
-                out=phi_s[g][:].bitcast(I32).rearrange("p t k q -> p k q t"),
-                in_=phi_s_raw[span][:, :, first : first + PASS].bitcast(I32).rearrange("p k (q t) -> p k q t", t=PACK),
+                out=scales[:].bitcast(I32).rearrange("p t k q -> p k q t"),
+                in_=phi_s_raw[part][:, :, first : first + PASS * (g1 - g0)].bitcast(I32).rearrange(
+                    "p k (q t) -> p k q t", t=PACK
+                ),
             )
+            for g in range(g0, g1):
+                phi_w[g] = words[:, :, :, 2 * P * (g - g0) : 2 * P * (g - g0 + 1)]
+                phi_s[g] = scales[:, :, :, P * (g - g0) : P * (g - g0 + 1)]
 
         def interleave(copy, grouped, raw, c0, c1):
             copy(
@@ -157,13 +169,13 @@ def tile_mppi_weighted_control_update_k5_kernel(
 
         def quantize(codes, scales, grouped):
             nc.vector.quantize_mx(
-                out=codes.bitcast(FP8X4), scales=scales, in_=grouped[:].rearrange("p c t -> p (c t)")
+                out=codes.bitcast(FP8X4), scales=scales, in_=grouped.rearrange("p c t -> p (c t)")
             )
 
-        eps_grouped, w_raw, w_grouped, update, squashed, y, y_turned, y_grouped = {}, {}, {}, {}, {}, {}, {}, {}
+        eps_grouped, w_raw, w_grouped, update, squashed, y, y_turned = {}, {}, {}, {}, {}, {}, {}
 
         def interleave_eps(h, g):
-            grouped = ring.tile([P, PASS, PACK], BF16, name="eps_grouped", align_bytes=64)
+            grouped = ring.tile([P, PASS, PACK], BF16, name="eps_grouped", bufs=4, align_bytes=64)
             split = SCALAR_COLS[GROUPS * h + g]
             if split > 0:
                 interleave(nc.scalar.copy, grouped, eps_raw[h][g], 0, split)
@@ -173,7 +185,7 @@ def tile_mppi_weighted_control_update_k5_kernel(
         def quantize_eps(h, g):
             eps_codes[h, g] = ring.tile([P, PASS], U32, name="eps_codes", bufs=4, align_bytes=64)
             eps_scales[h, g] = ring.tile([P, PASS], U8, name="eps_scales", bufs=4, align_bytes=64)
-            quantize(eps_codes[h, g][:], eps_scales[h, g][:], eps_grouped[h, g])
+            quantize(eps_codes[h, g][:], eps_scales[h, g][:], eps_grouped[h, g][:])
 
         def weights(g):
             raw = ring.tile([P, PACK, C], BF16, name="w_raw", align_bytes=64)
@@ -200,7 +212,7 @@ def tile_mppi_weighted_control_update_k5_kernel(
             w_grouped[g] = grouped
 
         def quantize_w(g):
-            quantize(w_codes[g][:], w_scales[g][:], w_grouped[g])
+            quantize(w_codes[g][:], w_scales[g][:], w_grouped[g][:])
 
         def accumulate(h, g):
             for m in range(C_TILES):
@@ -231,7 +243,7 @@ def tile_mppi_weighted_control_update_k5_kernel(
             nc.scalar.activation(out=squashed[h, m][:], in_=plan[:], func=ACT.Tanh)
 
         def scale_and_turn(h, m):
-            y[h, m] = kept("y%d_%d" % (h, m), [P, PASS], F32)
+            y[h, m] = ring.tile([P, PASS], F32, name="y", bufs=5)
             controls = slice(PASS * h, PASS * (h + 1))
             nc.vector.tensor_tensor(out=y[h, m][:], in0=squashed[h, m][:], in1=limit_sb[:, controls], op=ALU.mult)
             nc.sync.dma_start(out=out_0[P * m : P * (m + 1), controls], in_=y[h, m][:])
@@ -240,12 +252,13 @@ def tile_mppi_weighted_control_update_k5_kernel(
                 nc.tensor.transpose(y_turned[h, m][:, t, :], y[h, m][:, t:PASS:PACK], identity[:])
 
         def round_y(h, m):
-            y_grouped[h, m] = ring.tile([P, P, PACK], BF16, name="y_grouped", align_bytes=64)
-            nc.scalar.copy(out=y_grouped[h, m][:], in_=y_turned[h, m][:].rearrange("p t c -> p c t"))
+            nc.scalar.copy(
+                out=y_grouped[h][:, P * m : P * (m + 1), :], in_=y_turned[h, m][:].rearrange("p t c -> p c t")
+            )
 
-        def quantize_y(h, m):
-            goals = slice(P * m, P * (m + 1))
-            quantize(y_codes[h][:, goals], y_scales[h][:, goals], y_grouped[h, m])
+        def quantize_y(h, m0, m1):
+            goals = slice(P * m0, P * m1)
+            quantize(y_codes[h][:, goals], y_scales[h][:, goals], y_grouped[h][:, goals, :])
 
         def store_words(h, m0, m1):
             nc.sync.dma_start(
@@ -262,45 +275,42 @@ def tile_mppi_weighted_control_update_k5_kernel(
 
         permute_phi(0)
         nc.vector.tensor_copy(out=columns[:], in_=turned[:, :, 0:GROUPS])
-        accumulated = 0
-        for s in range(len(eps_order) + EPS_LAG):
-            e = s - EPS_LAG
-            m = e - GROUPS - EPILOGUE_LAG
+        chunks = len(eps_order)
+        tiles = [(h, m) for h in range(HALVES) for m in range(C_TILES)]
+        first_tile_step = chunks + LAG - C_TILES
+        permuted, accumulated = 1, 0
+        for s in range(first_tile_step + len(tiles) + 3):
+            e = s - LAG
+            i = s - first_tile_step
             if s < GROUPS:
                 weights(s)
-            if s + 1 < GROUPS:
-                permute_phi(s + 1)
-            if 0 <= m < C_TILES:
-                squash(0, m)
-            if e >= 0:
+            if permuted < len(PHI_SPANS) and PHI_SPANS[permuted][0] <= s + 2:
+                permute_phi(permuted)
+                permuted += 1
+            if 0 <= i < len(tiles):
+                squash(*tiles[i])
+            if 0 <= e < chunks:
                 quantize_eps(*eps_order[e])
             if 1 <= s <= GROUPS:
                 interleave_w(s - 1)
-            if 0 <= e + 1 < len(eps_order):
-                interleave_eps(*eps_order[e + 1])
-            if 1 <= s <= GROUPS:
-                quantize_w(s - 1)
-            while accumulated <= (e - 1 if s < GROUPS else e):
+            if s < chunks:
+                interleave_eps(*eps_order[s])
+            if LAG <= s < GROUPS + LAG:
+                quantize_w(e)
+            while accumulated <= min(chunks - 1, e - 1 if s < GROUPS else e):
                 accumulate(*eps_order[accumulated])
                 accumulated += 1
-            if 0 <= m < C_TILES:
-                scale_and_turn(0, m)
-            if 1 <= m <= C_TILES:
-                round_y(0, m - 1)
-            if m >= 2:
-                quantize_y(0, m - 2)
-        store_words(0, 0, C_TILES)
-        store_scales(0, [nc.sync])
-        for s in range(C_TILES + 3):
-            if s < C_TILES:
-                squash(1, s)
-            if 1 <= s <= C_TILES:
-                scale_and_turn(1, s - 1)
-            if 2 <= s <= C_TILES + 1:
-                round_y(1, s - 2)
-            if s >= 3:
-                quantize_y(1, s - 3)
-            if s == C_TILES + 1:
+            if 1 <= i <= len(tiles):
+                scale_and_turn(*tiles[i - 1])
+            if 2 <= i <= len(tiles) + 1:
+                round_y(*tiles[i - 2])
+            if i == C_TILES + 2:
+                quantize_y(0, 0, C_TILES)
+                store_words(0, 0, C_TILES)
+                store_scales(0, [nc.sync])
+            if i >= C_TILES + 3:
+                quantize_y(1, i - C_TILES - 3, i - C_TILES - 2)
+            if i == len(tiles) + 1:
                 store_words(1, 0, C_TILES - 1)
         store_words(1, C_TILES - 1, C_TILES)
         store_scales(1, [nc.scalar, nc.sync])

@@ -25,7 +25,8 @@ HALVES = D // PASS
 C_TILES = C // P
 EARLY_GROUPS = 3
 PHI_SPANS = [(0, 1), (1, 2), (2, 3), (3, 4), (4, 6), (6, 8)]
-SCALAR_COLS = [0, 64, 256, 256, 256, 256, 256, 256, 352, 352, 320, 320, 384, 352, 352, 320]
+SCALAR_COLS = [0, 0, 128, 256, 256, 256, 256, 256, 352, 352, 320, 320, 352, 256, 288, 288]
+FIRST_HALF_STEPS = [13, 15, 16, 17]
 LAG = 2
 
 
@@ -207,7 +208,7 @@ def tile_mppi_weighted_control_update_k5_kernel(
             w_raw[g] = raw
 
         def interleave_w(g):
-            grouped = ring.tile([P, C, PACK], BF16, name="w_grouped", align_bytes=64)
+            grouped = ring.tile([P, C, PACK], BF16, name="w_grouped", bufs=2, align_bytes=64)
             interleave(nc.vector.tensor_copy, grouped, w_raw[g], 0, C)
             w_grouped[g] = grouped
 
@@ -230,7 +231,7 @@ def tile_mppi_weighted_control_update_k5_kernel(
                 )
 
         def squash(h, m):
-            plan = ring.tile([P, PASS], F32, name="plan")
+            plan = ring.tile([P, PASS], F32, name="plan", bufs=4)
             nc.vector.scalar_tensor_tensor(
                 out=plan[:],
                 in0=update[h, m][:],
@@ -239,21 +240,45 @@ def tile_mppi_weighted_control_update_k5_kernel(
                 op0=ALU.mult,
                 op1=ALU.add,
             )
-            squashed[h, m] = ring.tile([P, PASS], F32, name="squashed")
+            squashed[h, m] = ring.tile([P, PASS], F32, name="squashed", bufs=5)
             nc.scalar.activation(out=squashed[h, m][:], in_=plan[:], func=ACT.Tanh)
 
-        def scale_and_turn(h, m):
+        def in_word_order(values):
+            return values.rearrange("c (p u e) -> c u p e", u=2, e=2)
+
+        def scale(h, m):
             y[h, m] = ring.tile([P, PASS], F32, name="y", bufs=5)
             controls = slice(PASS * h, PASS * (h + 1))
             nc.vector.tensor_tensor(out=y[h, m][:], in0=squashed[h, m][:], in1=limit_sb[:, controls], op=ALU.mult)
             nc.sync.dma_start(out=out_0[P * m : P * (m + 1), controls], in_=y[h, m][:])
-            y_turned[h, m] = bank(4 + m, [P, PACK, P])
-            for t in range(PACK):
-                nc.tensor.transpose(y_turned[h, m][:, t, :], y[h, m][:, t:PASS:PACK], identity[:])
 
-        def round_y(h, m):
+        def turn(h, m, pairs):
+            words = pairs[:].rearrange("c u p e -> c u (p e)").bitcast(F32)
+            y_turned[h, m] = bank(4 + m, [P, 2, P])
+            for u in range(2):
+                nc.tensor.transpose(y_turned[h, m][:, u, :], words[:, u, :], identity[:])
+
+        def scale_round_turn(h, m):
+            scale(h, m)
+            pairs = ring.tile([P, 2, P, 2], BF16, name="pairs", align_bytes=64)
+            nc.scalar.copy(out=pairs[:], in_=in_word_order(y[h, m][:]))
+            turn(h, m, pairs)
+
+        def round_turn_scale(h, m):
+            pairs = ring.tile([P, 2, P, 2], BF16, name="pairs", align_bytes=64)
+            nc.vector.tensor_tensor(
+                out=pairs[:],
+                in0=in_word_order(squashed[h, m][:]),
+                in1=in_word_order(limit_sb[:, PASS * h : PASS * (h + 1)]),
+                op=ALU.mult,
+            )
+            turn(h, m, pairs)
+            scale(h, m)
+
+        def group_y(h, m):
             nc.scalar.copy(
-                out=y_grouped[h][:, P * m : P * (m + 1), :], in_=y_turned[h, m][:].rearrange("p t c -> p c t")
+                out=y_grouped[h][:, P * m : P * (m + 1), :].bitcast(F32),
+                in_=y_turned[h, m][:].rearrange("p u c -> p c u"),
             )
 
         def quantize_y(h, m0, m1):
@@ -276,20 +301,19 @@ def tile_mppi_weighted_control_update_k5_kernel(
         permute_phi(0)
         nc.vector.tensor_copy(out=columns[:], in_=turned[:, :, 0:GROUPS])
         chunks = len(eps_order)
-        tiles = [(h, m) for h in range(HALVES) for m in range(C_TILES)]
-        first_tile_step = chunks + LAG - C_TILES
         permuted, accumulated = 1, 0
-        for s in range(first_tile_step + len(tiles) + 3):
+        for s in range(chunks + LAG):
             e = s - LAG
-            i = s - first_tile_step
             if s < GROUPS:
                 weights(s)
             if permuted < len(PHI_SPANS) and PHI_SPANS[permuted][0] <= s + 2:
                 permute_phi(permuted)
                 permuted += 1
-            if 0 <= i < len(tiles):
-                squash(*tiles[i])
-            if 0 <= e < chunks:
+            if s in FIRST_HALF_STEPS:
+                squash(0, FIRST_HALF_STEPS.index(s))
+            if 1 <= s <= LAG:
+                quantize_eps(*eps_order[s - 1])
+            if e >= LAG:
                 quantize_eps(*eps_order[e])
             if 1 <= s <= GROUPS:
                 interleave_w(s - 1)
@@ -297,20 +321,30 @@ def tile_mppi_weighted_control_update_k5_kernel(
                 interleave_eps(*eps_order[s])
             if LAG <= s < GROUPS + LAG:
                 quantize_w(e)
-            while accumulated <= min(chunks - 1, e - 1 if s < GROUPS else e):
+            while accumulated <= (e - 1 if s < GROUPS else e):
                 accumulate(*eps_order[accumulated])
                 accumulated += 1
-            if 1 <= i <= len(tiles):
-                scale_and_turn(*tiles[i - 1])
-            if 2 <= i <= len(tiles) + 1:
-                round_y(*tiles[i - 2])
-            if i == C_TILES + 2:
-                quantize_y(0, 0, C_TILES)
-                store_words(0, 0, C_TILES)
-                store_scales(0, [nc.sync])
-            if i >= C_TILES + 3:
-                quantize_y(1, i - C_TILES - 3, i - C_TILES - 2)
-            if i == len(tiles) + 1:
-                store_words(1, 0, C_TILES - 1)
-        store_words(1, C_TILES - 1, C_TILES)
+            if s - 1 in FIRST_HALF_STEPS:
+                scale_round_turn(0, FIRST_HALF_STEPS.index(s - 1))
+            if s - 2 in FIRST_HALF_STEPS:
+                group_y(0, FIRST_HALF_STEPS.index(s - 2))
+
+        squash(1, 0)
+        scale_round_turn(0, 3)
+        group_y(0, 2)
+        squash(1, 1)
+        squash(1, 2)
+        group_y(0, 3)
+        squash(1, 3)
+        for m in range(C_TILES - 1):
+            scale_round_turn(1, m)
+        quantize_y(0, 0, C_TILES)
+        store_words(0, 0, C_TILES)
+        store_scales(0, [nc.sync])
+        round_turn_scale(1, C_TILES - 1)
+        for m in range(C_TILES):
+            group_y(1, m)
+        for m0 in range(0, C_TILES, 2):
+            quantize_y(1, m0, m0 + 2)
+            store_words(1, m0, m0 + 2)
         store_scales(1, [nc.scalar, nc.sync])

from contextlib import ExitStack

import concourse.mybir as mybir
from concourse.masks import make_identity

R, K, C, D = 4096, 1024, 512, 1024
FLOPS = 2 * R * K * C + 2 * R * C * D

F32 = mybir.dt.float32
BF16 = mybir.dt.bfloat16
I32 = mybir.dt.int32
U32 = mybir.dt.uint32
U8 = mybir.dt.uint8
FP8X4 = mybir.dt.float8_e4m3fn_x4
FP4X4 = mybir.dt.float4_e2m1fn_x4
ACT = mybir.ActivationFunctionType
ALU = mybir.AluOpType

P = 128
PACK = 4
PASS = P * PACK
K_PASSES = K // PASS
GROUPS = R // PASS
HALVES = D // PASS
C_TILES = C // P
EARLY_GROUPS = 3
PHI_SPANS = [(0, 1), (1, 2), (2, 3), (3, 4), (4, 6), (6, 8)]
SCALAR_COLS = [0, 0, 128, 256, 256, 256, 256, 256, 352, 352, 320, 320, 352, 256, 288, 288]
FIRST_HALF_STEPS = [13, 15, 16, 17]
LAG = 2


def tile_mppi_weighted_control_update_k5_kernel(
    tc, phi_words, phi_scales, theta_words, theta_scales, rollout_factor, eps, step, nominal, limit,
    out_0, out_1, out_2,
):
    nc = tc.nc
    with ExitStack() as ctx:
        keep = ctx.enter_context(tc.tile_pool(name="keep", bufs=1))
        ring = ctx.enter_context(tc.tile_pool(name="ring", bufs=3))
        psum = ctx.enter_context(tc.psum_pool(name="psum", bufs=1))
        ctx.enter_context(tc.manual_schedule())

        def kept(name, shape, dtype):
            return keep.tile(shape, dtype, name=name, align_bytes=64)

        def bank(index, shape):
            return psum.tile(shape, F32, name="bank%d" % index)

        theta_w = kept("theta_w", [P, K_PASSES, 2 * C], U8)
        theta_s = kept("theta_s", [P, K_PASSES, C], U8)
        scale_spans = [(0, EARLY_GROUPS), (EARLY_GROUPS, GROUPS)]
        phi_s_raw = [
            kept("phi_s_raw%d" % i, [P, K_PASSES, (g1 - g0) * PASS], U8) for i, (g0, g1) in enumerate(scale_spans)
        ]
        phi_w_raw = [
            kept("phi_w_raw%d" % g0, [P, K_PASSES, 2 * PASS * (g1 - g0)], U8) for g0, g1 in PHI_SPANS
        ]
        eps_raw = [[kept("eps_raw%d_%d" % (h, g), [P, PACK, PASS], BF16) for g in range(GROUPS)] for h in range(HALVES)]
        w_codes = [kept("w_codes%d" % g, [P, C], U32) for g in range(GROUPS)]
        w_scales = [kept("w_scales%d" % g, [P, C], U8) for g in range(GROUPS)]
        nominal_sb = [kept("nominal_sb%d" % h, [P, C_TILES, PASS], BF16) for h in range(HALVES)]
        limit_sb = kept("limit_sb", [P, D], BF16)
        y_codes = [kept("y_codes%d" % h, [P, C], U32) for h in range(HALVES)]
        y_scales = [kept("y_scales%d" % h, [P, C], U8) for h in range(HALVES)]
        y_grouped = [kept("y_grouped%d" % h, [P, C, PACK], BF16) for h in range(HALVES)]
        small_raw = kept("small_raw", [P, PASS], BF16)
        rows = kept("rows", [P, PACK, P], F32)
        columns = kept("columns", [P, PACK, GROUPS], F32)
        step_sb = kept("step_sb", [P, C_TILES, 2], BF16)
        identity = kept("identity", [P, P], F32)
        warm = kept("warm", [P, 2], F32)

        nc.vector.memset(warm[:, 0:1], 1.0)
        nc.vector.memset(phi_s_raw[0][:].rearrange("p k n -> p (k n)").bitcast(I32), 0)
        nc.vector.memset(theta_s[:].rearrange("p k n -> p (k n)").bitcast(I32), 0)
        nc.vector.memset(rows[:], 0.0)
        nc.vector.memset(phi_s_raw[1][:].rearrange("p k n -> p (k n)").bitcast(I32), 0)

        def load_scale_rows(plane, source):
            for quadrant in range(4):
                nc.sync.dma_start(
                    out=plane[32 * quadrant : 32 * quadrant + 4, :, :].bitcast(I32),
                    in_=source[:, 4 * quadrant : 4 * quadrant + 4, :].rearrange("k r n -> r k n").bitcast(I32),
                )

        def load_phi_words(i):
            g0, g1 = PHI_SPANS[i]
            nc.sync.dma_start(
                out=phi_w_raw[i][:].bitcast(I32),
                in_=phi_words[:, :, 2 * PASS * g0 : 2 * PASS * g1].rearrange("k p n -> p k n").bitcast(I32),
            )

        def load_eps(h, g):
            source = eps[PASS * g : PASS * (g + 1), PASS * h : PASS * (h + 1)].rearrange(
                "(q t j) d -> j q t d", t=PACK, j=4
            )
            for j in range(4):
                nc.sync.dma_start(out=eps_raw[h][g][j:P:4, :, :], in_=source[j])

        def load_nominal(h):
            nc.sync.dma_start(
                out=nominal_sb[h][:], in_=nominal[:, PASS * h : PASS * (h + 1)].rearrange("(m p) d -> p m d", p=P)
            )

        make_identity(nc, identity[:])
        eps_order = [(h, g) for h in range(HALVES) for g in range(GROUPS)]
        nc.sync.dma_start(out=small_raw[0:GROUPS, :], in_=rollout_factor.rearrange("(g n) -> g n", g=GROUPS))
        load_phi_words(0)
        load_scale_rows(phi_s_raw[0], phi_scales[:, :, 0 : EARLY_GROUPS * PASS])
        nc.sync.dma_start(out=theta_w[:].bitcast(I32), in_=theta_words.rearrange("k p n -> p k n").bitcast(I32))
        load_scale_rows(theta_s, theta_scales)
        load_phi_words(1)
        phi_before = {1: 2, 2: 3, 3: 4, 5: 5}
        for e, (h, g) in enumerate(eps_order):
            if e == 2:
                load_scale_rows(phi_s_raw[1], phi_scales[:, :, EARLY_GROUPS * PASS :])
            if e in phi_before:
                load_phi_words(phi_before[e])
            if e == GROUPS + 1:
                load_nominal(0)
                with nc.allow_non_contiguous_dma(reason="one step value for each partition"):
                    nc.sync.dma_start(out=step_sb[:, :, 0:1], in_=step.rearrange("(m p o) -> p m o", p=P, o=1))
                nc.sync.dma_start(out=limit_sb[:], in_=limit.partition_broadcast(P))
            load_eps(h, g)
        load_nominal(1)

        nc.scalar.activation(out=warm[:, 1:2], in_=warm[:, 0:1], func=ACT.Ln)
        nc.scalar.activation(
            out=rows[0:GROUPS, :, :].rearrange("g t (q j) -> g t q j", j=4),
            in_=small_raw[0:GROUPS, :].rearrange("g (q t j) -> g t q j", t=PACK, j=4),
            func=ACT.Ln,
        )
        nc.scalar.activation(out=warm[:, 1:2], in_=warm[:, 0:1], func=ACT.Exp)
        turned = bank(4, [P, PACK, P])
        for t in range(PACK):
            nc.tensor.transpose(turned[:, t, :], rows[:, t, :], identity[:])

        phi_w, phi_s, eps_codes, eps_scales = {}, {}, {}, {}

        def permute_phi(i):
            g0, g1 = PHI_SPANS[i]
            words = ring.tile([P, PACK, K_PASSES, 2 * P * (g1 - g0)], U8, name="phi_w", align_bytes=64)
            scales = ring.tile([P, PACK, K_PASSES, P * (g1 - g0)], U8, name="phi_s", align_bytes=64)
            nc.vector.tensor_copy(
                out=words[:].rearrange("p t k n -> p (t k n)").bitcast(I32).rearrange(
                    "p (t u w) -> p u t w", t=PACK, w=2
                ),
                in_=phi_w_raw[i][:].rearrange("p k n -> p (k n)").bitcast(I32).rearrange(
                    "p (u t w) -> p u t w", t=PACK, w=2
                ),
            )
            part = 0 if g0 < EARLY_GROUPS else 1
            first = (g0 - scale_spans[part][0]) * PASS
            nc.vector.tensor_copy(
                out=scales[:].bitcast(I32).rearrange("p t k q -> p k q t"),
                in_=phi_s_raw[part][:, :, first : first + PASS * (g1 - g0)].bitcast(I32).rearrange(
                    "p k (q t) -> p k q t", t=PACK
                ),
            )
            for g in range(g0, g1):
                phi_w[g] = words[:, :, :, 2 * P * (g - g0) : 2 * P * (g - g0 + 1)]
                phi_s[g] = scales[:, :, :, P * (g - g0) : P * (g - g0 + 1)]

        def interleave(copy, grouped, raw, c0, c1):
            copy(
                out=grouped[:, c0:c1, :].rearrange("p (c i) t -> p c t i", i=4),
                in_=raw[:, :, c0:c1].rearrange("p t (c i) -> p c t i", i=4),
            )

        def quantize(codes, scales, grouped):
            nc.vector.quantize_mx(
                out=codes.bitcast(FP8X4), scales=scales, in_=grouped.rearrange("p c t -> p (c t)")
            )

        eps_grouped, w_raw, w_grouped, update, squashed, y, y_turned = {}, {}, {}, {}, {}, {}, {}

        def interleave_eps(h, g):
            grouped = ring.tile([P, PASS, PACK], BF16, name="eps_grouped", bufs=4, align_bytes=64)
            split = SCALAR_COLS[GROUPS * h + g]
            if split > 0:
                interleave(nc.scalar.copy, grouped, eps_raw[h][g], 0, split)
            interleave(nc.vector.tensor_copy, grouped, eps_raw[h][g], split, PASS)
            eps_grouped[h, g] = grouped

        def quantize_eps(h, g):
            eps_codes[h, g] = ring.tile([P, PASS], U32, name="eps_codes", bufs=4, align_bytes=64)
            eps_scales[h, g] = ring.tile([P, PASS], U8, name="eps_scales", bufs=4, align_bytes=64)
            quantize(eps_codes[h, g][:], eps_scales[h, g][:], eps_grouped[h, g][:])

        def weights(g):
            raw = ring.tile([P, PACK, C], BF16, name="w_raw", align_bytes=64)
            for t in range(PACK):
                cost = bank(t, [P, C])
                for k in range(K_PASSES):
                    nc.tensor.matmul_mx(
                        out=cost[:],
                        lhsT=phi_w[g][:, t, k, :].bitcast(FP4X4),
                        lhsT_scale=phi_s[g][:, t, k, :],
                        rhs=theta_w[:, k, :].bitcast(FP4X4),
                        rhs_scale=theta_s[:, k, :],
                        start=(k == 0),
                        stop=(k == K_PASSES - 1),
                    )
                nc.scalar.activation(
                    out=raw[:, t, :], in_=cost[:], func=ACT.Exp, scale=-1.0, bias=columns[:, t, g : g + 1]
                )
            w_raw[g] = raw

        def interleave_w(g):
            grouped = ring.tile([P, C, PACK], BF16, name="w_grouped", bufs=2, align_bytes=64)
            interleave(nc.vector.tensor_copy, grouped, w_raw[g], 0, C)
            w_grouped[g] = grouped

        def quantize_w(g):
            quantize(w_codes[g][:], w_scales[g][:], w_grouped[g][:])

        def accumulate(h, g):
            for m in range(C_TILES):
                if g == 0:
                    update[h, m] = bank(m + 4 * (1 - h), [P, PASS])
                goals = slice(P * m, P * (m + 1))
                nc.tensor.matmul_mx(
                    out=update[h, m][:],
                    lhsT=w_codes[g][:, goals].bitcast(FP8X4),
                    lhsT_scale=w_scales[g][:, goals],
                    rhs=eps_codes[h, g][:].bitcast(FP8X4),
                    rhs_scale=eps_scales[h, g][:],
                    start=(g == 0),
                    stop=(g == GROUPS - 1),
                )

        def squash(h, m):
            plan = ring.tile([P, PASS], F32, name="plan", bufs=4)
            nc.vector.scalar_tensor_tensor(
                out=plan[:],
                in0=update[h, m][:],
                scalar=step_sb[:, m, 0:1],
                in1=nominal_sb[h][:, m, :],
                op0=ALU.mult,
                op1=ALU.add,
            )
            squashed[h, m] = ring.tile([P, PASS], F32, name="squashed", bufs=5)
            nc.scalar.activation(out=squashed[h, m][:], in_=plan[:], func=ACT.Tanh)

        def in_word_order(values):
            return values.rearrange("c (p u e) -> c u p e", u=2, e=2)

        def scale(h, m):
            y[h, m] = ring.tile([P, PASS], F32, name="y", bufs=5)
            controls = slice(PASS * h, PASS * (h + 1))
            nc.vector.tensor_tensor(out=y[h, m][:], in0=squashed[h, m][:], in1=limit_sb[:, controls], op=ALU.mult)
            nc.sync.dma_start(out=out_0[P * m : P * (m + 1), controls], in_=y[h, m][:])

        def turn(h, m, pairs):
            words = pairs[:].rearrange("c u p e -> c u (p e)").bitcast(F32)
            y_turned[h, m] = bank(4 + m, [P, 2, P])
            for u in range(2):
                nc.tensor.transpose(y_turned[h, m][:, u, :], words[:, u, :], identity[:])

        def scale_round_turn(h, m):
            scale(h, m)
            pairs = ring.tile([P, 2, P, 2], BF16, name="pairs", align_bytes=64)
            nc.scalar.copy(out=pairs[:], in_=in_word_order(y[h, m][:]))
            turn(h, m, pairs)

        def round_turn_scale(h, m):
            pairs = ring.tile([P, 2, P, 2], BF16, name="pairs", align_bytes=64)
            nc.vector.tensor_tensor(
                out=pairs[:],
                in0=in_word_order(squashed[h, m][:]),
                in1=in_word_order(limit_sb[:, PASS * h : PASS * (h + 1)]),
                op=ALU.mult,
            )
            turn(h, m, pairs)
            scale(h, m)

        def group_y(h, m):
            nc.scalar.copy(
                out=y_grouped[h][:, P * m : P * (m + 1), :].bitcast(F32),
                in_=y_turned[h, m][:].rearrange("p u c -> p c u"),
            )

        def quantize_y(h, m0, m1):
            goals = slice(P * m0, P * m1)
            quantize(y_codes[h][:, goals], y_scales[h][:, goals], y_grouped[h][:, goals, :])

        def store_words(h, m0, m1):
            nc.sync.dma_start(
                out=out_1[h, :, P * m0 : P * m1, :].rearrange("p m t -> p (m t)").bitcast(I32),
                in_=y_codes[h][:, P * m0 : P * m1].bitcast(I32),
            )

        def store_scales(h, queues):
            for quadrant in range(4):
                queues[quadrant % len(queues)].dma_start(
                    out=out_2[h, 4 * quadrant : 4 * quadrant + 4, :].bitcast(I32),
                    in_=y_scales[h][32 * quadrant : 32 * quadrant + 4, :].bitcast(I32),
                )

        permute_phi(0)
        nc.vector.tensor_copy(out=columns[:], in_=turned[:, :, 0:GROUPS])
        chunks = len(eps_order)
        permuted, accumulated = 1, 0
        for s in range(chunks + LAG):
            e = s - LAG
            if s < GROUPS:
                weights(s)
            if permuted < len(PHI_SPANS) and PHI_SPANS[permuted][0] <= s + 2:
                permute_phi(permuted)
                permuted += 1
            if s in FIRST_HALF_STEPS:
                squash(0, FIRST_HALF_STEPS.index(s))
            if 1 <= s <= LAG:
                quantize_eps(*eps_order[s - 1])
            if e >= LAG:
                quantize_eps(*eps_order[e])
            if 1 <= s <= GROUPS:
                interleave_w(s - 1)
            if s < chunks:
                interleave_eps(*eps_order[s])
            if LAG <= s < GROUPS + LAG:
                quantize_w(e)
            while accumulated <= (e - 1 if s < GROUPS else e):
                accumulate(*eps_order[accumulated])
                accumulated += 1
            if s - 1 in FIRST_HALF_STEPS:
                scale_round_turn(0, FIRST_HALF_STEPS.index(s - 1))
            if s - 2 in FIRST_HALF_STEPS:
                group_y(0, FIRST_HALF_STEPS.index(s - 2))

        squash(1, 0)
        scale_round_turn(0, 3)
        group_y(0, 2)
        squash(1, 1)
        squash(1, 2)
        group_y(0, 3)
        squash(1, 3)
        for m in range(C_TILES - 1):
            scale_round_turn(1, m)
        quantize_y(0, 0, C_TILES)
        store_words(0, 0, C_TILES)
        store_scales(0, [nc.sync])
        round_turn_scale(1, C_TILES - 1)
        for m in range(C_TILES):
            group_y(1, m)
        for m0 in range(0, C_TILES, 2):
            quantize_y(1, m0, m0 + 2)
            store_words(1, m0, m0 + 2)
        store_scales(1, [nc.scalar, nc.sync])
